import numpy as np
import ml_dtypes


def mxq(x, axis, fmt="e4m3"):
    dtype, down = {"e4m3": (ml_dtypes.float8_e4m3fn, 7), "e5m2": (ml_dtypes.float8_e5m2, 14)}[fmt]
    v = np.moveaxis(np.asarray(x, np.float32).astype(ml_dtypes.bfloat16).astype(np.float64), axis, -1)
    blocks = v.reshape(v.shape[:-1] + (-1, 32))
    amax = np.abs(blocks).max(-1, keepdims=True)
    byte = np.maximum(np.where(amax > 0, np.frexp(amax)[1] - 1 + 127, 0) - down, 1)
    scale = np.exp2(byte - 127.0)
    codes = (blocks / scale).astype(np.float32).astype(dtype).astype(np.float64)
    return np.moveaxis((codes * scale).reshape(v.shape), -1, axis)


WIDE = False


def mx_kscale(k):
    if not WIDE:
        return np.ones(k)
    levels = np.array([10, -10, 5, -5, 0])
    if k % 512:
        return np.exp2(np.random.permutation(np.resize(levels, k // 32))).repeat(32)
    a = np.empty((k // 512, 16))
    for p in range(k // 512):
        a[p, :8] = np.random.permutation(np.resize(levels, 8))
        for g in range(8):
            far = levels[np.abs(levels - a[p, g]) >= 10]
            a[p, g + 8] = far[np.random.randint(len(far))]
    return np.exp2(a.ravel()).repeat(32)


def f64(x):
    return np.asarray(x).astype(np.float64)


def striped(idx):
    return np.tile(idx.reshape(-1, 16).T, (8, 1)).astype(np.uint16)


def unstriped(offs):
    return offs[:16].T.reshape(-1).astype(np.int64)


def pack_weight(w):
    k, n = w.shape
    w = f64(np.asarray(w, np.float32).astype(ml_dtypes.bfloat16)).reshape(k // 32, 32, n)
    amax = np.abs(w).max(1)
    byte = np.clip(np.where(amax > 0, np.frexp(amax)[1] - 1 + 127 - 7, 1), 1, 254)
    scaled = (w * np.exp2(127.0 - byte)[:, None, :]).reshape(k, n).astype(np.float32)
    words = np.ascontiguousarray(scaled.reshape(k // 512, 128, 4, n).transpose(0, 1, 3, 2)).astype(ml_dtypes.float8_e4m3fn).view(np.uint8)
    return words, np.ascontiguousarray(byte.astype(np.uint8).reshape(k // 512, 16, n))


def unpack_weight(words, scales):
    g, p, n, _ = words.shape
    vals = np.ascontiguousarray(words).view(ml_dtypes.float8_e4m3fn).astype(np.float64) * np.repeat(np.exp2(scales.astype(np.float64) - 127.0), 8, axis=1)[..., None]
    return vals.transpose(0, 1, 3, 2).reshape(g * 512, n)


def sigmoid(v):
    return 1.0 / (1.0 + np.exp(-np.maximum(v, -700.0)))


K, T, S, H, C = 512, 2048, 512, 512, 512


def setup_inputs():
    n = np.random.standard_normal
    s = mx_kscale(K)[:, None]
    packed_xT = pack_weight(n((K, T)) * s)
    return {
        "x_words": packed_xT[0],
        "x_scales": packed_xT[1],
        "w1": (n((K, H)) / np.sqrt(K) / s).astype(np.float32),
        "sl": np.random.uniform(1.0, 2.0, (H, 1)).astype(np.float32),
        "th": (0.5 * n((H, 1))).astype(np.float32),
        "gs": (np.random.uniform(0.5, 1.5, (K, 1)) / s).astype(np.float32),
        "wb": (n((K, S)) / np.sqrt(K) / s).astype(np.float32),
        "sl2": np.random.uniform(1.0, 2.0, (C, 1)).astype(np.float32),
        "th2": (0.5 * n((C, 1))).astype(np.float32),
        "offs": striped(np.random.permutation(T)[:S]),
        "n1": striped(np.random.permutation(S)),
        "n2": striped(np.random.permutation(S)),
        "n3": striped(np.random.permutation(S)),
        "cand": striped(np.random.permutation(T)[:C]),
        "cb": striped(np.random.permutation(T)[:C]),
        "n4": striped(np.random.permutation(S)),
        "n5": striped(np.random.permutation(S)),
    }


def reference(x_words, x_scales, w1, sl, th, gs, wb, sl2, th2, offs, n1, n2, n3, cand, cb, n4, n5):
    x_cand = unpack_weight(x_words, x_scales)[:, unstriped(cand)]
    xq = unpack_weight(x_words, x_scales)[:, unstriped(offs)]
    y = mxq(f64(w1), 0, "e4m3").T @ xq
    own = sigmoid(f64(sl) * (y - f64(th)))
    sg = sigmoid(f64(sl) * (y[:, unstriped(n1)] - f64(th)))
    z = f64(gs) * (y[:, unstriped(n2)] * own + y[:, unstriped(n3)] * sg)
    a = 0.0625 * ((x_cand.T @ mxq(z, 0, "e4m3")))
    x_cb = unpack_weight(x_words, x_scales)[:, unstriped(cb)]
    b = x_cb.T @ mxq(f64(wb), 0, "e4m3")
    sg2 = sigmoid(f64(sl2) * (b[:, unstriped(n4)] - f64(th2)))
    return np.maximum(a * sg2, b[:, unstriped(n5)] - b)

@@ -1,0 +1,183 @@
+from contextlib import ExitStack
+
+import concourse.mybir as mybir
+
+K, T, S, H, C = 512, 2048, 512, 512, 512
+FLOPS = 2 * K * H * S + 2 * H * C * S + 2 * K * C * S
+
+F32 = mybir.dt.float32
+BF16 = mybir.dt.bfloat16
+I32 = mybir.dt.int32
+U32 = mybir.dt.uint32
+U16 = mybir.dt.uint16
+U8 = mybir.dt.uint8
+FP8X4 = mybir.dt.float8_e4m3fn_x4
+ALU = mybir.AluOpType
+ACT = mybir.ActivationFunctionType
+
+P = 128
+PACK = 4
+HALF = S // 2
+
+
+def tile_picked_cdswmxbemx_none_p_kernel(
+    tc, x_words, x_scales, w1, sl, th, gs, wb, sl2, th2, offs, n1, n2, n3, cand, cb, n4, n5, out
+):
+    nc = tc.nc
+    with ExitStack() as ctx:
+        keep = ctx.enter_context(tc.tile_pool(name="keep", bufs=1))
+        psum = ctx.enter_context(tc.psum_pool(name="psum", bufs=1))
+
+        def load_list(src, name):
+            dst = keep.tile([P, S // 16], U16, name=name)
+            nc.sync.dma_start(dst[:], src)
+            return dst
+
+        def load_column(src, name, pattern):
+            dst = keep.tile([P, PACK], F32, name=name)
+            with nc.allow_non_contiguous_dma(reason="one value a row of the result"):
+                nc.sync.dma_start(out=dst[:], in_=src.rearrange(pattern, p=P))
+            return dst
+
+        def mx_tiles(name, words_tag=None, scale_tag=None):
+            words = keep.tile([P, S], U32, name=name + "_words", tag=words_tag or name + "_words", align_bytes=64)
+            scale = keep.tile([P, S], U8, name=name + "_scale", tag=scale_tag or name + "_scale", align_bytes=64)
+            return words, scale
+
+        xs = keep.tile([P, T], U8, name="xs", align_bytes=64)
+        nc.gpsimd.memset(xs[:].bitcast(I32), 0)
+        w1_raw = keep.tile([P, PACK, H], F32, name="w1_raw")
+        nc.sync.dma_start(out=w1_raw[:], in_=w1.rearrange("(p j) c -> p j c", j=PACK))
+        offs_t = load_list(offs, "offs_t")
+        for q in range(4):
+            nc.sync.dma_start(out=xs[32 * q : 32 * q + 4, :].bitcast(I32), in_=x_scales[0, 4 * q : 4 * q + 4, :].bitcast(I32))
+        xw = keep.tile([P, T], U32, name="xw", align_bytes=64)
+        nc.sync.dma_start(out=xw[:].bitcast(I32), in_=x_words[0].rearrange("p n t -> p (n t)").bitcast(I32))
+        cb_t = load_list(cb, "cb_t")
+        sl_t = load_column(sl, "sl_t", "(p t) o -> p (t o)")
+        th_t = load_column(th, "th_t", "(p t) o -> p (t o)")
+        n1_t = load_list(n1, "n1_t")
+        n2_t = load_list(n2, "n2_t")
+        gs_t = load_column(gs, "gs_t", "(p t) o -> p (t o)")
+        n3_t = load_list(n3, "n3_t")
+        wb_raw = keep.tile([P, PACK, S], F32, name="wb_raw")
+        nc.sync.dma_start(out=wb_raw[:], in_=wb.rearrange("(p j) c -> p j c", j=PACK))
+        cand_t = load_list(cand, "cand_t")
+        n4_t = load_list(n4, "n4_t")
+        n5_t = load_list(n5, "n5_t")
+        sl2_t = load_column(sl2, "sl2_t", "(t p) o -> p (t o)")
+        th2_t = load_column(th2, "th2_t", "(t p) o -> p (t o)")
+
+        xq_w, xq_s = mx_tiles("xq", "picked_words", "picked_scale")
+        w1_w, w1_s = mx_tiles("w1")
+        wb_w, wb_s = mx_tiles("wb")
+        z_w, z_s = mx_tiles("z")
+
+        nc.vector.tensor_copy(xq_s[:], xs[:].indirect(offs_t[:]))
+        w1_g = keep.tile([P, H * PACK], BF16, name="w1_g", align_bytes=64)
+        w1_dst = w1_g[:].rearrange("p (t m j) -> p m j t", t=PACK, j=PACK)
+        w1_src = w1_raw[:].rearrange("p j (m t) -> p m j t", t=PACK)
+        nc.scalar.copy(out=w1_dst[:, :80], in_=w1_src[:, :80])
+        nc.vector.tensor_copy(out=w1_dst[:, 80:], in_=w1_src[:, 80:])
+        nc.vector.quantize_mx(out=w1_w[:].bitcast(FP8X4), scales=w1_s[:], in_=w1_g[:])
+        y_ps = [psum.tile([P, S], F32, name=f"y_ps{t}", tag=f"ya{t}") for t in range(PACK)]
+        for h in range(2):
+            cols = slice(h * HALF, (h + 1) * HALF)
+            nc.vector.tensor_copy(xq_w[:, cols], xw[:].indirect(offs_t[:, h * HALF // 16 : (h + 1) * HALF // 16]))
+            for t in range(PACK):
+                rows = slice(t * P, (t + 1) * P)
+                nc.tensor.matmul_mx(
+                    out=y_ps[t][:, cols], lhsT=w1_w[:, rows].bitcast(FP8X4), lhsT_scale=w1_s[:, rows],
+                    rhs=xq_w[:, cols].bitcast(FP8X4), rhs_scale=xq_s[:, cols], start=True, stop=True,
+                )
+        nb = keep.tile([P, PACK], F32, name="nb")
+        nc.vector.scalar_tensor_tensor(nb[:], sl_t[:], -1.0, th_t[:], ALU.mult, ALU.mult)
+
+        y_win = [keep.tile([P, 2 * S], F32, name=f"y_win{t}") for t in range(PACK)]
+        g_win = [keep.tile([P, 2 * S], F32, name=f"g_win{t}") for t in range(PACK)]
+        b_win = [keep.tile([P, 2 * S], F32, name=f"b_win{t}") for t in range(PACK)]
+        t1 = keep.tile([P, PACK, S], F32, name="t1")
+        t2 = keep.tile([P, PACK, S], F32, name="t2")
+
+        for t in range(PACK):
+            col = slice(t, t + 1)
+            if t == 0:
+                for h in range(2):
+                    cols = slice(h * HALF, (h + 1) * HALF)
+                    nc.scalar.copy(out=y_win[t][:, cols], in_=y_ps[t][:, cols])
+            else:
+                nc.vector.tensor_copy(y_win[t][:, :S], y_ps[t][:])
+            nc.vector.tensor_scalar(g_win[t][:, :S], y_win[t][:, :S], gs_t[:, col], None, ALU.mult)
+        for t in range(PACK):
+            col = slice(t, t + 1)
+            nc.scalar.activation(y_win[t][:, S:], y_win[t][:, :S], ACT.Sigmoid, bias=nb[:, col], scale=sl_t[:, col])
+            nc.scalar.activation(b_win[t][:, S:], y_win[t][:].indirect(n1_t[:]), ACT.Sigmoid, bias=nb[:, col], scale=sl_t[:, col])
+            nc.scalar.activation(g_win[t][:, S:], y_win[t][:].indirect(n2_t[:]), ACT.Copy)
+
+        xb_w = keep.tile([P, S], U32, name="xb_w", tag="picked_words", align_bytes=64)
+        xb_s = keep.tile([P, S], U8, name="xb_s", align_bytes=64)
+        nc.vector.tensor_copy(xb_s[:], xs[:].indirect(cb_t[:]))
+        nc.vector.tensor_copy(xb_w[:], xw[:].indirect(cb_t[:]))
+        wb_g = keep.tile([P, S * PACK], BF16, name="wb_g", align_bytes=64)
+
+        def z_plane(t):
+            col = slice(t, t + 1)
+            nc.vector.tensor_tensor(t2[:, t, :], g_win[t][:].indirect(n3_t[:]), b_win[t][:, S:], ALU.mult)
+            nc.vector.scalar_tensor_tensor(t1[:, t, :], g_win[t][:, S:], gs_t[:, col], y_win[t][:, S:], ALU.mult, ALU.mult)
+
+        z_plane(0)
+        nc.vector.tensor_copy(
+            wb_g[:].rearrange("p (c i j) -> p c j i", i=4, j=PACK),
+            wb_raw[:].rearrange("p j (c i) -> p c j i", i=4),
+        )
+        z_plane(1)
+        nc.vector.quantize_mx(out=wb_w[:].bitcast(FP8X4), scales=wb_s[:], in_=wb_g[:])
+        b_ps = [psum.tile([P, S], F32, name=f"b_ps{t}") for t in range(PACK)]
+        for t in range(PACK):
+            rows = slice(t * P, (t + 1) * P)
+            nc.tensor.matmul_mx(
+                out=b_ps[t][:], lhsT=xb_w[:, rows].bitcast(FP8X4), lhsT_scale=xb_s[:, rows],
+                rhs=wb_w[:].bitcast(FP8X4), rhs_scale=wb_s[:], start=True, stop=True,
+            )
+        xc_w, xc_s = mx_tiles("xc", "picked_words", "picked_scale")
+        nc.vector.tensor_copy(xc_s[:], xs[:].indirect(cand_t[:]))
+        nb2 = keep.tile([P, PACK], F32, name="nb2")
+        nc.vector.scalar_tensor_tensor(nb2[:], sl2_t[:], -1.0, th2_t[:], ALU.mult, ALU.mult)
+        z_plane(2)
+        nc.vector.tensor_copy(xc_w[:], xw[:].indirect(cand_t[:]))
+        z_plane(3)
+
+        z_g = keep.tile([P, S * PACK], BF16, name="z_g", align_bytes=64)
+        a_ps = [psum.tile([P, S], F32, name=f"a_ps{t}", tag=f"ya{t}") for t in range(PACK)]
+        for h in range(2):
+            cols = slice(h * HALF, (h + 1) * HALF)
+            nc.vector.tensor_tensor(
+                z_g[:, h * HALF * PACK : (h + 1) * HALF * PACK].rearrange("p (c i t) -> p c t i", i=2, t=PACK),
+                t1[:, :, cols].rearrange("p t (c i) -> p c t i", i=2),
+                t2[:, :, cols].rearrange("p t (c i) -> p c t i", i=2), ALU.add,
+            )
+        for h in range(2):
+            cols = slice(h * HALF, (h + 1) * HALF)
+            nc.vector.quantize_mx(out=z_w[:, cols].bitcast(FP8X4), scales=z_s[:, cols], in_=z_g[:, h * HALF * PACK : (h + 1) * HALF * PACK])
+            for t in range(PACK):
+                rows = slice(t * P, (t + 1) * P)
+                nc.tensor.matmul_mx(
+                    out=a_ps[t][:, cols], lhsT=xc_w[:, rows].bitcast(FP8X4), lhsT_scale=xc_s[:, rows],
+                    rhs=z_w[:, cols].bitcast(FP8X4), rhs_scale=z_s[:, cols], start=True, stop=True,
+                )
+
+        for t in range(PACK):
+            col = slice(t, t + 1)
+            b5 = keep.tile([P, S], F32, name=f"b5_{t}")
+            sg2 = keep.tile([P, S], F32, name=f"sg2_{t}")
+            diff = keep.tile([P, S], F32, name=f"diff{t}")
+            prod = keep.tile([P, S], F32, name=f"prod{t}")
+            res = keep.tile([P, S], F32, name=f"res{t}")
+            if t >= 0:
+                nc.scalar.copy(out=b_win[t][:, :S], in_=b_ps[t][:])
+            nc.scalar.activation(b5[:], b_win[t][:].indirect(n5_t[:]), ACT.Copy)
+            nc.scalar.activation(sg2[:], b_win[t][:].indirect(n4_t[:]), ACT.Sigmoid, bias=nb2[:, col], scale=sl2_t[:, col])
+            nc.vector.tensor_tensor(diff[:], b5[:], b_win[t][:, :S], ALU.subtract)
+            nc.vector.scalar_tensor_tensor(prod[:], a_ps[t][:], 0.0625, sg2[:], ALU.mult, ALU.mult)
+            nc.vector.tensor_tensor(res[:], prod[:], diff[:], ALU.max)
+            nc.sync.dma_start(out=out[t * P : (t + 1) * P, :], in_=res[:])

@@ -33,16 +33,23 @@ def tile_picked_cdswmxbemx_none_p_kernel(
             nc.sync.dma_start(dst[:], src)
             return dst
 
-        def load_column(src, name, pattern):
+        def load_column(src, name, pattern, queue):
             dst = keep.tile([P, PACK], F32, name=name)
             with nc.allow_non_contiguous_dma(reason="one value a row of the result"):
-                nc.sync.dma_start(out=dst[:], in_=src.rearrange(pattern, p=P))
+                queue.dma_start(out=dst[:], in_=src.rearrange(pattern, p=P))
             return dst
 
         def mx_tiles(name, words_tag=None, scale_tag=None):
             words = keep.tile([P, S], U32, name=name + "_words", tag=words_tag or name + "_words", align_bytes=64)
             scale = keep.tile([P, S], U8, name=name + "_scale", tag=scale_tag or name + "_scale", align_bytes=64)
             return words, scale
+
+        def neg_product(slope, threshold, name):
+            both = keep.tile([P, PACK], F32, name=name + "_pos")
+            neg = keep.tile([P, PACK], F32, name=name)
+            nc.gpsimd.tensor_tensor(both[:], slope[:], threshold[:], ALU.mult)
+            nc.gpsimd.tensor_scalar(neg[:], both[:], -1.0, 0.0, ALU.mult, ALU.add)
+            return neg
 
         xs = keep.tile([P, T], U8, name="xs", align_bytes=64)
         nc.gpsimd.memset(xs[:].bitcast(I32), 0)
@@ -54,19 +61,19 @@ def tile_picked_cdswmxbemx_none_p_kernel(
         xw = keep.tile([P, T], U32, name="xw", align_bytes=64)
         nc.sync.dma_start(out=xw[:].bitcast(I32), in_=x_words[0].rearrange("p n t -> p (n t)").bitcast(I32))
         cb_t = load_list(cb, "cb_t")
-        sl_t = load_column(sl, "sl_t", "(p t) o -> p (t o)")
-        th_t = load_column(th, "th_t", "(p t) o -> p (t o)")
+        sl_t = load_column(sl, "sl_t", "(p t) o -> p (t o)", nc.gpsimd)
+        th_t = load_column(th, "th_t", "(p t) o -> p (t o)", nc.gpsimd)
         n1_t = load_list(n1, "n1_t")
         n2_t = load_list(n2, "n2_t")
-        gs_t = load_column(gs, "gs_t", "(p t) o -> p (t o)")
+        gs_t = load_column(gs, "gs_t", "(p t) o -> p (t o)", nc.sync)
         n3_t = load_list(n3, "n3_t")
         wb_raw = keep.tile([P, PACK, S], F32, name="wb_raw")
         nc.sync.dma_start(out=wb_raw[:], in_=wb.rearrange("(p j) c -> p j c", j=PACK))
         cand_t = load_list(cand, "cand_t")
         n4_t = load_list(n4, "n4_t")
         n5_t = load_list(n5, "n5_t")
-        sl2_t = load_column(sl2, "sl2_t", "(t p) o -> p (t o)")
-        th2_t = load_column(th2, "th2_t", "(t p) o -> p (t o)")
+        sl2_t = load_column(sl2, "sl2_t", "(t p) o -> p (t o)", nc.sync)
+        th2_t = load_column(th2, "th2_t", "(t p) o -> p (t o)", nc.sync)
 
         xq_w, xq_s = mx_tiles("xq", "picked_words", "picked_scale")
         w1_w, w1_s = mx_tiles("w1")
@@ -77,21 +84,24 @@ def tile_picked_cdswmxbemx_none_p_kernel(
         w1_g = keep.tile([P, H * PACK], BF16, name="w1_g", align_bytes=64)
         w1_dst = w1_g[:].rearrange("p (t m j) -> p m j t", t=PACK, j=PACK)
         w1_src = w1_raw[:].rearrange("p j (m t) -> p m j t", t=PACK)
-        nc.scalar.copy(out=w1_dst[:, :80], in_=w1_src[:, :80])
-        nc.vector.tensor_copy(out=w1_dst[:, 80:], in_=w1_src[:, 80:])
-        nc.vector.quantize_mx(out=w1_w[:].bitcast(FP8X4), scales=w1_s[:], in_=w1_g[:])
+        nc.scalar.copy(out=w1_dst[:, :96], in_=w1_src[:, :96])
+        nc.vector.tensor_copy(out=w1_dst[:, 96:], in_=w1_src[:, 96:])
+        nc.vector.quantize_mx(out=w1_w[:, :P].bitcast(FP8X4), scales=w1_s[:, :P], in_=w1_g[:, : P * PACK])
         y_ps = [psum.tile([P, S], F32, name=f"y_ps{t}", tag=f"ya{t}") for t in range(PACK)]
+        y_first = psum.tile([P, S], F32, name="y_first", tag="b3")
         for h in range(2):
             cols = slice(h * HALF, (h + 1) * HALF)
             nc.vector.tensor_copy(xq_w[:, cols], xw[:].indirect(offs_t[:, h * HALF // 16 : (h + 1) * HALF // 16]))
-            for t in range(PACK):
-                rows = slice(t * P, (t + 1) * P)
+        nc.vector.quantize_mx(out=w1_w[:, P:].bitcast(FP8X4), scales=w1_s[:, P:], in_=w1_g[:, P * PACK :])
+        for t in range(PACK):
+            rows = slice(t * P, (t + 1) * P)
+            for h in range(2):
+                cols = slice(h * HALF, (h + 1) * HALF)
                 nc.tensor.matmul_mx(
-                    out=y_ps[t][:, cols], lhsT=w1_w[:, rows].bitcast(FP8X4), lhsT_scale=w1_s[:, rows],
+                    out=(y_first if (t, h) == (0, 0) else y_ps[t])[:, cols], lhsT=w1_w[:, rows].bitcast(FP8X4), lhsT_scale=w1_s[:, rows],
                     rhs=xq_w[:, cols].bitcast(FP8X4), rhs_scale=xq_s[:, cols], start=True, stop=True,
                 )
-        nb = keep.tile([P, PACK], F32, name="nb")
-        nc.vector.scalar_tensor_tensor(nb[:], sl_t[:], -1.0, th_t[:], ALU.mult, ALU.mult)
+        nb = neg_product(sl_t, th_t, "nb")
 
         y_win = [keep.tile([P, 2 * S], F32, name=f"y_win{t}") for t in range(PACK)]
         g_win = [keep.tile([P, 2 * S], F32, name=f"g_win{t}") for t in range(PACK)]
@@ -99,18 +109,19 @@ def tile_picked_cdswmxbemx_none_p_kernel(
         t1 = keep.tile([P, PACK, S], F32, name="t1")
         t2 = keep.tile([P, PACK, S], F32, name="t2")
 
+        for t in range(1, PACK):
+            nc.vector.tensor_copy(y_win[t][:, :S], y_ps[t][:])
         for t in range(PACK):
             col = slice(t, t + 1)
             if t == 0:
                 for h in range(2):
                     cols = slice(h * HALF, (h + 1) * HALF)
-                    nc.scalar.copy(out=y_win[t][:, cols], in_=y_ps[t][:, cols])
+                    bank = y_first if h == 0 else y_ps[0]
+                    nc.scalar.activation(y_win[t][:, S + h * HALF : S + (h + 1) * HALF], bank[:, cols], ACT.Sigmoid, bias=nb[:, col], scale=sl_t[:, col])
+                    nc.scalar.copy(out=y_win[t][:, cols], in_=bank[:, cols])
             else:
-                nc.vector.tensor_copy(y_win[t][:, :S], y_ps[t][:])
+                nc.scalar.activation(y_win[t][:, S:], y_win[t][:, :S], ACT.Sigmoid, bias=nb[:, col], scale=sl_t[:, col])
             nc.vector.tensor_scalar(g_win[t][:, :S], y_win[t][:, :S], gs_t[:, col], None, ALU.mult)
-        for t in range(PACK):
-            col = slice(t, t + 1)
-            nc.scalar.activation(y_win[t][:, S:], y_win[t][:, :S], ACT.Sigmoid, bias=nb[:, col], scale=sl_t[:, col])
             nc.scalar.activation(b_win[t][:, S:], y_win[t][:].indirect(n1_t[:]), ACT.Sigmoid, bias=nb[:, col], scale=sl_t[:, col])
             nc.scalar.activation(g_win[t][:, S:], y_win[t][:].indirect(n2_t[:]), ACT.Copy)
 
@@ -132,7 +143,7 @@ def tile_picked_cdswmxbemx_none_p_kernel(
         )
         z_plane(1)
         nc.vector.quantize_mx(out=wb_w[:].bitcast(FP8X4), scales=wb_s[:], in_=wb_g[:])
-        b_ps = [psum.tile([P, S], F32, name=f"b_ps{t}") for t in range(PACK)]
+        b_ps = [psum.tile([P, S], F32, name=f"b_ps{t}", tag=f"b{t}") for t in range(PACK)]
         for t in range(PACK):
             rows = slice(t * P, (t + 1) * P)
             nc.tensor.matmul_mx(
@@ -141,8 +152,7 @@ def tile_picked_cdswmxbemx_none_p_kernel(
             )
         xc_w, xc_s = mx_tiles("xc", "picked_words", "picked_scale")
         nc.vector.tensor_copy(xc_s[:], xs[:].indirect(cand_t[:]))
-        nb2 = keep.tile([P, PACK], F32, name="nb2")
-        nc.vector.scalar_tensor_tensor(nb2[:], sl2_t[:], -1.0, th2_t[:], ALU.mult, ALU.mult)
+        nb2 = neg_product(sl2_t, th2_t, "nb2")
         z_plane(2)
         nc.vector.tensor_copy(xc_w[:], xw[:].indirect(cand_t[:]))
         z_plane(3)
@@ -166,18 +176,28 @@ def tile_picked_cdswmxbemx_none_p_kernel(
                     rhs=z_w[:, cols].bitcast(FP8X4), rhs_scale=z_s[:, cols], start=True, stop=True,
                 )
 
-        for t in range(PACK):
+        b5 = [keep.tile([P, S], F32, name=f"b5_{t}") for t in range(PACK)]
+        sg2 = [keep.tile([P, S], F32, name=f"sg2_{t}") for t in range(PACK)]
+        diff = [keep.tile([P, S], F32, name=f"diff{t}") for t in range(PACK)]
+        prod = [keep.tile([P, S], F32, name=f"prod{t}") for t in range(PACK)]
+        res = [keep.tile([P, S], F32, name=f"res{t}") for t in range(PACK)]
+        pieces = [(t, slice(0, S)) for t in range(PACK - 1)] + [(PACK - 1, slice(0, HALF)), (PACK - 1, slice(HALF, S))]
+
+        def finish(t, cols):
+            nc.vector.tensor_tensor(res[t][:, cols], prod[t][:, cols], diff[t][:, cols], ALU.max)
+            nc.sync.dma_start(out=out[t * P : (t + 1) * P, cols], in_=res[t][:, cols])
+
+        for n, (t, cols) in enumerate(pieces):
             col = slice(t, t + 1)
-            b5 = keep.tile([P, S], F32, name=f"b5_{t}")
-            sg2 = keep.tile([P, S], F32, name=f"sg2_{t}")
-            diff = keep.tile([P, S], F32, name=f"diff{t}")
-            prod = keep.tile([P, S], F32, name=f"prod{t}")
-            res = keep.tile([P, S], F32, name=f"res{t}")
-            if t >= 0:
+            if cols.start == 0:
                 nc.scalar.copy(out=b_win[t][:, :S], in_=b_ps[t][:])
-            nc.scalar.activation(b5[:], b_win[t][:].indirect(n5_t[:]), ACT.Copy)
-            nc.scalar.activation(sg2[:], b_win[t][:].indirect(n4_t[:]), ACT.Sigmoid, bias=nb2[:, col], scale=sl2_t[:, col])
-            nc.vector.tensor_tensor(diff[:], b5[:], b_win[t][:, :S], ALU.subtract)
-            nc.vector.scalar_tensor_tensor(prod[:], a_ps[t][:], 0.0625, sg2[:], ALU.mult, ALU.mult)
-            nc.vector.tensor_tensor(res[:], prod[:], diff[:], ALU.max)
-            nc.sync.dma_start(out=out[t * P : (t + 1) * P, :], in_=res[:])
+                nc.scalar.activation(b5[t][:], b_win[t][:].indirect(n5_t[:]), ACT.Copy)
+                nc.vector.tensor_tensor(diff[t][:], b5[t][:], b_win[t][:, :S], ALU.subtract)
+                if n > 0:
+                    finish(*pieces[n - 1])
+            places = n4_t[:, cols.start // 16 : cols.stop // 16]
+            nc.scalar.activation(sg2[t][:, cols], b_win[t][:].indirect(places), ACT.Sigmoid, bias=nb2[:, col], scale=sl2_t[:, col])
+            nc.vector.scalar_tensor_tensor(prod[t][:, cols], a_ps[t][:, cols], 0.0625, sg2[t][:, cols], ALU.mult, ALU.mult)
+            if cols.start > 0:
+                finish(*pieces[n - 1])
+        finish(*pieces[-1])

@@ -56,8 +56,8 @@ def tile_picked_cdswmxbemx_none_p_kernel(
         w1_raw = keep.tile([P, PACK, H], F32, name="w1_raw")
         nc.sync.dma_start(out=w1_raw[:], in_=w1.rearrange("(p j) c -> p j c", j=PACK))
         offs_t = load_list(offs, "offs_t")
-        for q in range(4):
-            nc.sync.dma_start(out=xs[32 * q : 32 * q + 4, :].bitcast(I32), in_=x_scales[0, 4 * q : 4 * q + 4, :].bitcast(I32))
+        for r in range(4):
+            nc.sync.dma_start(out=xs[r:P:32, :].bitcast(I32), in_=x_scales[0, r:16:4, :].bitcast(I32))
         xw = keep.tile([P, T], U32, name="xw", align_bytes=64)
         nc.sync.dma_start(out=xw[:].bitcast(I32), in_=x_words[0].rearrange("p n t -> p (n t)").bitcast(I32))
         cb_t = load_list(cb, "cb_t")
@@ -65,11 +65,11 @@ def tile_picked_cdswmxbemx_none_p_kernel(
         th_t = load_column(th, "th_t", "(p t) o -> p (t o)", nc.gpsimd)
         n1_t = load_list(n1, "n1_t")
         n2_t = load_list(n2, "n2_t")
+        cand_t = load_list(cand, "cand_t")
         gs_t = load_column(gs, "gs_t", "(p t) o -> p (t o)", nc.sync)
         n3_t = load_list(n3, "n3_t")
         wb_raw = keep.tile([P, PACK, S], F32, name="wb_raw")
         nc.sync.dma_start(out=wb_raw[:], in_=wb.rearrange("(p j) c -> p j c", j=PACK))
-        cand_t = load_list(cand, "cand_t")
         n4_t = load_list(n4, "n4_t")
         n5_t = load_list(n5, "n5_t")
         sl2_t = load_column(sl2, "sl2_t", "(t p) o -> p (t o)", nc.sync)
@@ -104,10 +104,11 @@ def tile_picked_cdswmxbemx_none_p_kernel(
         nb = neg_product(sl_t, th_t, "nb")
 
         y_win = [keep.tile([P, 2 * S], F32, name=f"y_win{t}") for t in range(PACK)]
-        g_win = [keep.tile([P, 2 * S], F32, name=f"g_win{t}") for t in range(PACK)]
+        y2 = [keep.tile([P, S], F32, name=f"y2_{t}") for t in range(PACK)]
         b_win = [keep.tile([P, 2 * S], F32, name=f"b_win{t}") for t in range(PACK)]
-        t1 = keep.tile([P, PACK, S], F32, name="t1")
-        t2 = keep.tile([P, PACK, S], F32, name="t2")
+        t1 = [keep.tile([P, S], F32, name=f"t1_{t}") for t in range(PACK)]
+        t2 = [keep.tile([P, S], F32, name=f"t2_{t}") for t in range(PACK)]
+        z_rows = keep.tile([P, PACK, S], BF16, name="z_rows", align_bytes=64)
 
         for t in range(1, PACK):
             nc.vector.tensor_copy(y_win[t][:, :S], y_ps[t][:])
@@ -121,9 +122,8 @@ def tile_picked_cdswmxbemx_none_p_kernel(
                     nc.scalar.copy(out=y_win[t][:, cols], in_=bank[:, cols])
             else:
                 nc.scalar.activation(y_win[t][:, S:], y_win[t][:, :S], ACT.Sigmoid, bias=nb[:, col], scale=sl_t[:, col])
-            nc.vector.tensor_scalar(g_win[t][:, :S], y_win[t][:, :S], gs_t[:, col], None, ALU.mult)
             nc.scalar.activation(b_win[t][:, S:], y_win[t][:].indirect(n1_t[:]), ACT.Sigmoid, bias=nb[:, col], scale=sl_t[:, col])
-            nc.scalar.activation(g_win[t][:, S:], y_win[t][:].indirect(n2_t[:]), ACT.Copy)
+            nc.scalar.activation(y2[t][:], y_win[t][:].indirect(n2_t[:]), ACT.Copy)
 
         xb_w = keep.tile([P, S], U32, name="xb_w", tag="picked_words", align_bytes=64)
         xb_s = keep.tile([P, S], U8, name="xb_s", align_bytes=64)
@@ -133,15 +133,18 @@ def tile_picked_cdswmxbemx_none_p_kernel(
 
         def z_plane(t):
             col = slice(t, t + 1)
-            nc.vector.tensor_tensor(t2[:, t, :], g_win[t][:].indirect(n3_t[:]), b_win[t][:, S:], ALU.mult)
-            nc.vector.scalar_tensor_tensor(t1[:, t, :], g_win[t][:, S:], gs_t[:, col], y_win[t][:, S:], ALU.mult, ALU.mult)
+            nc.vector.tensor_tensor(t2[t][:], y_win[t][:].indirect(n3_t[:]), b_win[t][:, S:], ALU.mult)
+            nc.vector.scalar_tensor_tensor(t1[t][:], y2[t][:], gs_t[:, col], y_win[t][:, S:], ALU.mult, ALU.mult)
 
-        z_plane(0)
+        def z_sum(t):
+            nc.vector.scalar_tensor_tensor(z_rows[:, t, :], t2[t][:], gs_t[:, t : t + 1], t1[t][:], ALU.mult, ALU.add)
+
+        xc_s = keep.tile([P, S], U8, name="xc_s", tag="picked_scale", align_bytes=64)
+        nc.vector.tensor_copy(xc_s[:], xs[:].indirect(cand_t[:]))
         nc.vector.tensor_copy(
             wb_g[:].rearrange("p (c i j) -> p c j i", i=4, j=PACK),
             wb_raw[:].rearrange("p j (c i) -> p c j i", i=4),
         )
-        z_plane(1)
         nc.vector.quantize_mx(out=wb_w[:].bitcast(FP8X4), scales=wb_s[:], in_=wb_g[:])
         b_ps = [psum.tile([P, S], F32, name=f"b_ps{t}", tag=f"b{t}") for t in range(PACK)]
         for t in range(PACK):
@@ -150,21 +153,22 @@ def tile_picked_cdswmxbemx_none_p_kernel(
                 out=b_ps[t][:], lhsT=xb_w[:, rows].bitcast(FP8X4), lhsT_scale=xb_s[:, rows],
                 rhs=wb_w[:].bitcast(FP8X4), rhs_scale=wb_s[:], start=True, stop=True,
             )
-        xc_w, xc_s = mx_tiles("xc", "picked_words", "picked_scale")
-        nc.vector.tensor_copy(xc_s[:], xs[:].indirect(cand_t[:]))
-        nb2 = neg_product(sl2_t, th2_t, "nb2")
-        z_plane(2)
+        xc_w = keep.tile([P, S], U32, name="xc_w", align_bytes=64)
         nc.vector.tensor_copy(xc_w[:], xw[:].indirect(cand_t[:]))
-        z_plane(3)
+        nb2 = neg_product(sl2_t, th2_t, "nb2")
+        for t in range(PACK):
+            z_plane(t)
+            if t > 0:
+                z_sum(t - 1)
+        z_sum(PACK - 1)
 
         z_g = keep.tile([P, S * PACK], BF16, name="z_g", align_bytes=64)
         a_ps = [psum.tile([P, S], F32, name=f"a_ps{t}", tag=f"ya{t}") for t in range(PACK)]
         for h in range(2):
             cols = slice(h * HALF, (h + 1) * HALF)
-            nc.vector.tensor_tensor(
-                z_g[:, h * HALF * PACK : (h + 1) * HALF * PACK].rearrange("p (c i t) -> p c t i", i=2, t=PACK),
-                t1[:, :, cols].rearrange("p t (c i) -> p c t i", i=2),
-                t2[:, :, cols].rearrange("p t (c i) -> p c t i", i=2), ALU.add,
+            nc.vector.tensor_copy(
+                z_g[:, h * HALF * PACK : (h + 1) * HALF * PACK].rearrange("p (c i t) -> p c t i", i=4, t=PACK),
+                z_rows[:, :, cols].rearrange("p t (c i) -> p c t i", i=4),
             )
         for h in range(2):
             cols = slice(h * HALF, (h + 1) * HALF)
@@ -178,26 +182,43 @@ def tile_picked_cdswmxbemx_none_p_kernel(
 
         b5 = [keep.tile([P, S], F32, name=f"b5_{t}") for t in range(PACK)]
         sg2 = [keep.tile([P, S], F32, name=f"sg2_{t}") for t in range(PACK)]
-        diff = [keep.tile([P, S], F32, name=f"diff{t}") for t in range(PACK)]
         prod = [keep.tile([P, S], F32, name=f"prod{t}") for t in range(PACK)]
         res = [keep.tile([P, S], F32, name=f"res{t}") for t in range(PACK)]
-        pieces = [(t, slice(0, S)) for t in range(PACK - 1)] + [(PACK - 1, slice(0, HALF)), (PACK - 1, slice(HALF, S))]
+        diff = {}
+        whole, halves = slice(0, S), (slice(0, HALF), slice(HALF, S))
+
+        def fetch(t, parts):
+            col = slice(t, t + 1)
+            nc.scalar.copy(out=b_win[t][:, :S], in_=b_ps[t][:])
+            nc.scalar.activation(b5[t][:], b_win[t][:].indirect(n5_t[:]), ACT.Copy)
+            for cols in parts:
+                places = n4_t[:, cols.start // 16 : cols.stop // 16]
+                nc.scalar.activation(sg2[t][:, cols], b_win[t][:].indirect(places), ACT.Sigmoid, bias=nb2[:, col], scale=sl2_t[:, col])
+
+        def subtract(t):
+            diff[t] = keep.tile([P, S], F32, name=f"diff{t}", tag=f"diff{t % 2}")
+            nc.vector.tensor_tensor(diff[t][:], b5[t][:], b_win[t][:, :S], ALU.subtract)
+
+        def multiply(t, cols):
+            nc.vector.scalar_tensor_tensor(prod[t][:, cols], a_ps[t][:, cols], 0.0625, sg2[t][:, cols], ALU.mult, ALU.mult)
 
         def finish(t, cols):
             nc.vector.tensor_tensor(res[t][:, cols], prod[t][:, cols], diff[t][:, cols], ALU.max)
             nc.sync.dma_start(out=out[t * P : (t + 1) * P, cols], in_=res[t][:, cols])
 
-        for n, (t, cols) in enumerate(pieces):
-            col = slice(t, t + 1)
-            if cols.start == 0:
-                nc.scalar.copy(out=b_win[t][:, :S], in_=b_ps[t][:])
-                nc.scalar.activation(b5[t][:], b_win[t][:].indirect(n5_t[:]), ACT.Copy)
-                nc.vector.tensor_tensor(diff[t][:], b5[t][:], b_win[t][:, :S], ALU.subtract)
-                if n > 0:
-                    finish(*pieces[n - 1])
-            places = n4_t[:, cols.start // 16 : cols.stop // 16]
-            nc.scalar.activation(sg2[t][:, cols], b_win[t][:].indirect(places), ACT.Sigmoid, bias=nb2[:, col], scale=sl2_t[:, col])
-            nc.vector.scalar_tensor_tensor(prod[t][:, cols], a_ps[t][:, cols], 0.0625, sg2[t][:, cols], ALU.mult, ALU.mult)
-            if cols.start > 0:
-                finish(*pieces[n - 1])
-        finish(*pieces[-1])
+        for t in range(PACK):
+            fetch(t, halves if t == PACK - 1 else (whole,))
+        subtract(0)
+        subtract(1)
+        multiply(0, whole)
+        multiply(1, whole)
+        finish(0, whole)
+        subtract(2)
+        finish(1, whole)
+        multiply(2, whole)
+        subtract(3)
+        finish(2, whole)
+        for cols in halves:
+            multiply(3, cols)
+        for cols in halves:
+            finish(3, cols)

from contextlib import ExitStack

import concourse.mybir as mybir

K, T, S, H, C = 512, 2048, 512, 512, 512
FLOPS = 2 * K * H * S + 2 * H * C * S + 2 * K * C * S

F32 = mybir.dt.float32
BF16 = mybir.dt.bfloat16
I32 = mybir.dt.int32
U32 = mybir.dt.uint32
U16 = mybir.dt.uint16
U8 = mybir.dt.uint8
FP8X4 = mybir.dt.float8_e4m3fn_x4
ALU = mybir.AluOpType
ACT = mybir.ActivationFunctionType

P = 128
PACK = 4
HALF = S // 2


def tile_picked_cdswmxbemx_none_p_kernel(
    tc, x_words, x_scales, w1, sl, th, gs, wb, sl2, th2, offs, n1, n2, n3, cand, cb, n4, n5, out
):
    nc = tc.nc
    with ExitStack() as ctx:
        keep = ctx.enter_context(tc.tile_pool(name="keep", bufs=1))
        psum = ctx.enter_context(tc.psum_pool(name="psum", bufs=1))

        def load_list(src, name):
            dst = keep.tile([P, S // 16], U16, name=name)
            nc.sync.dma_start(dst[:], src)
            return dst

        def load_column(src, name, pattern, queue):
            dst = keep.tile([P, PACK], F32, name=name)
            with nc.allow_non_contiguous_dma(reason="one value a row of the result"):
                queue.dma_start(out=dst[:], in_=src.rearrange(pattern, p=P))
            return dst

        def mx_tiles(name, words_tag=None, scale_tag=None):
            words = keep.tile([P, S], U32, name=name + "_words", tag=words_tag or name + "_words", align_bytes=64)
            scale = keep.tile([P, S], U8, name=name + "_scale", tag=scale_tag or name + "_scale", align_bytes=64)
            return words, scale

        def neg_product(slope, threshold, name):
            both = keep.tile([P, PACK], F32, name=name + "_pos")
            neg = keep.tile([P, PACK], F32, name=name)
            nc.gpsimd.tensor_tensor(both[:], slope[:], threshold[:], ALU.mult)
            nc.gpsimd.tensor_scalar(neg[:], both[:], -1.0, 0.0, ALU.mult, ALU.add)
            return neg

        xs = keep.tile([P, T], U8, name="xs", align_bytes=64)
        nc.gpsimd.memset(xs[:].bitcast(I32), 0)
        w1_raw = keep.tile([P, PACK, H], F32, name="w1_raw")
        nc.sync.dma_start(out=w1_raw[:], in_=w1.rearrange("(p j) c -> p j c", j=PACK))
        offs_t = load_list(offs, "offs_t")
        for r in range(4):
            nc.sync.dma_start(out=xs[r:P:32, :].bitcast(I32), in_=x_scales[0, r:16:4, :].bitcast(I32))
        xw = keep.tile([P, T], U32, name="xw", align_bytes=64)
        nc.sync.dma_start(out=xw[:].bitcast(I32), in_=x_words[0].rearrange("p n t -> p (n t)").bitcast(I32))
        cb_t = load_list(cb, "cb_t")
        sl_t = load_column(sl, "sl_t", "(p t) o -> p (t o)", nc.gpsimd)
        th_t = load_column(th, "th_t", "(p t) o -> p (t o)", nc.gpsimd)
        n1_t = load_list(n1, "n1_t")
        n2_t = load_list(n2, "n2_t")
        cand_t = load_list(cand, "cand_t")
        gs_t = load_column(gs, "gs_t", "(p t) o -> p (t o)", nc.sync)
        n3_t = load_list(n3, "n3_t")
        wb_raw = keep.tile([P, PACK, S], F32, name="wb_raw")
        nc.sync.dma_start(out=wb_raw[:], in_=wb.rearrange("(p j) c -> p j c", j=PACK))
        n4_t = load_list(n4, "n4_t")
        n5_t = load_list(n5, "n5_t")
        sl2_t = load_column(sl2, "sl2_t", "(t p) o -> p (t o)", nc.sync)
        th2_t = load_column(th2, "th2_t", "(t p) o -> p (t o)", nc.sync)

        xq_w, xq_s = mx_tiles("xq", "picked_words", "picked_scale")
        w1_w, w1_s = mx_tiles("w1")
        wb_w, wb_s = mx_tiles("wb")
        z_w, z_s = mx_tiles("z")

        nc.vector.tensor_copy(xq_s[:], xs[:].indirect(offs_t[:]))
        w1_g = keep.tile([P, H * PACK], BF16, name="w1_g", align_bytes=64)
        w1_dst = w1_g[:].rearrange("p (t m j) -> p m j t", t=PACK, j=PACK)
        w1_src = w1_raw[:].rearrange("p j (m t) -> p m j t", t=PACK)
        nc.scalar.copy(out=w1_dst[:, :96], in_=w1_src[:, :96])
        nc.vector.tensor_copy(out=w1_dst[:, 96:], in_=w1_src[:, 96:])
        nc.vector.quantize_mx(out=w1_w[:, :P].bitcast(FP8X4), scales=w1_s[:, :P], in_=w1_g[:, : P * PACK])
        y_ps = [psum.tile([P, S], F32, name=f"y_ps{t}", tag=f"ya{t}") for t in range(PACK)]
        y_first = psum.tile([P, S], F32, name="y_first", tag="b3")
        for h in range(2):
            cols = slice(h * HALF, (h + 1) * HALF)
            nc.vector.tensor_copy(xq_w[:, cols], xw[:].indirect(offs_t[:, h * HALF // 16 : (h + 1) * HALF // 16]))
        nc.vector.quantize_mx(out=w1_w[:, P:].bitcast(FP8X4), scales=w1_s[:, P:], in_=w1_g[:, P * PACK :])
        for t in range(PACK):
            rows = slice(t * P, (t + 1) * P)
            for h in range(2):
                cols = slice(h * HALF, (h + 1) * HALF)
                nc.tensor.matmul_mx(
                    out=(y_first if (t, h) == (0, 0) else y_ps[t])[:, cols], lhsT=w1_w[:, rows].bitcast(FP8X4), lhsT_scale=w1_s[:, rows],
                    rhs=xq_w[:, cols].bitcast(FP8X4), rhs_scale=xq_s[:, cols], start=True, stop=True,
                )
        nb = neg_product(sl_t, th_t, "nb")

        y_win = [keep.tile([P, 2 * S], F32, name=f"y_win{t}") for t in range(PACK)]
        y2 = [keep.tile([P, S], F32, name=f"y2_{t}") for t in range(PACK)]
        b_win = [keep.tile([P, 2 * S], F32, name=f"b_win{t}") for t in range(PACK)]
        t1 = [keep.tile([P, S], F32, name=f"t1_{t}") for t in range(PACK)]
        t2 = [keep.tile([P, S], F32, name=f"t2_{t}") for t in range(PACK)]
        z_rows = keep.tile([P, PACK, S], BF16, name="z_rows", align_bytes=64)

        for t in range(1, PACK):
            nc.vector.tensor_copy(y_win[t][:, :S], y_ps[t][:])
        for t in range(PACK):
            col = slice(t, t + 1)
            if t == 0:
                for h in range(2):
                    cols = slice(h * HALF, (h + 1) * HALF)
                    bank = y_first if h == 0 else y_ps[0]
                    nc.scalar.activation(y_win[t][:, S + h * HALF : S + (h + 1) * HALF], bank[:, cols], ACT.Sigmoid, bias=nb[:, col], scale=sl_t[:, col])
                    nc.scalar.copy(out=y_win[t][:, cols], in_=bank[:, cols])
            else:
                nc.scalar.activation(y_win[t][:, S:], y_win[t][:, :S], ACT.Sigmoid, bias=nb[:, col], scale=sl_t[:, col])
            nc.scalar.activation(b_win[t][:, S:], y_win[t][:].indirect(n1_t[:]), ACT.Sigmoid, bias=nb[:, col], scale=sl_t[:, col])
            nc.scalar.activation(y2[t][:], y_win[t][:].indirect(n2_t[:]), ACT.Copy)

        xb_w = keep.tile([P, S], U32, name="xb_w", tag="picked_words", align_bytes=64)
        xb_s = keep.tile([P, S], U8, name="xb_s", align_bytes=64)
        nc.vector.tensor_copy(xb_s[:], xs[:].indirect(cb_t[:]))
        nc.vector.tensor_copy(xb_w[:], xw[:].indirect(cb_t[:]))
        wb_g = keep.tile([P, S * PACK], BF16, name="wb_g", align_bytes=64)

        def z_plane(t):
            col = slice(t, t + 1)
            nc.vector.tensor_tensor(t2[t][:], y_win[t][:].indirect(n3_t[:]), b_win[t][:, S:], ALU.mult)
            nc.vector.scalar_tensor_tensor(t1[t][:], y2[t][:], gs_t[:, col], y_win[t][:, S:], ALU.mult, ALU.mult)

        def z_sum(t):
            nc.vector.scalar_tensor_tensor(z_rows[:, t, :], t2[t][:], gs_t[:, t : t + 1], t1[t][:], ALU.mult, ALU.add)

        xc_s = keep.tile([P, S], U8, name="xc_s", tag="picked_scale", align_bytes=64)
        nc.vector.tensor_copy(xc_s[:], xs[:].indirect(cand_t[:]))
        nc.vector.tensor_copy(
            wb_g[:].rearrange("p (c i j) -> p c j i", i=4, j=PACK),
            wb_raw[:].rearrange("p j (c i) -> p c j i", i=4),
        )
        nc.vector.quantize_mx(out=wb_w[:].bitcast(FP8X4), scales=wb_s[:], in_=wb_g[:])
        b_ps = [psum.tile([P, S], F32, name=f"b_ps{t}", tag=f"b{t}") for t in range(PACK)]
        for t in range(PACK):
            rows = slice(t * P, (t + 1) * P)
            nc.tensor.matmul_mx(
                out=b_ps[t][:], lhsT=xb_w[:, rows].bitcast(FP8X4), lhsT_scale=xb_s[:, rows],
                rhs=wb_w[:].bitcast(FP8X4), rhs_scale=wb_s[:], start=True, stop=True,
            )
        xc_w = keep.tile([P, S], U32, name="xc_w", align_bytes=64)
        nc.vector.tensor_copy(xc_w[:], xw[:].indirect(cand_t[:]))
        nb2 = neg_product(sl2_t, th2_t, "nb2")
        for t in range(PACK):
            z_plane(t)
            if t > 0:
                z_sum(t - 1)
        z_sum(PACK - 1)

        z_g = keep.tile([P, S * PACK], BF16, name="z_g", align_bytes=64)
        a_ps = [psum.tile([P, S], F32, name=f"a_ps{t}", tag=f"ya{t}") for t in range(PACK)]
        for h in range(2):
            cols = slice(h * HALF, (h + 1) * HALF)
            nc.vector.tensor_copy(
                z_g[:, h * HALF * PACK : (h + 1) * HALF * PACK].rearrange("p (c i t) -> p c t i", i=4, t=PACK),
                z_rows[:, :, cols].rearrange("p t (c i) -> p c t i", i=4),
            )
        for h in range(2):
            cols = slice(h * HALF, (h + 1) * HALF)
            nc.vector.quantize_mx(out=z_w[:, cols].bitcast(FP8X4), scales=z_s[:, cols], in_=z_g[:, h * HALF * PACK : (h + 1) * HALF * PACK])
            for t in range(PACK):
                rows = slice(t * P, (t + 1) * P)
                nc.tensor.matmul_mx(
                    out=a_ps[t][:, cols], lhsT=xc_w[:, rows].bitcast(FP8X4), lhsT_scale=xc_s[:, rows],
                    rhs=z_w[:, cols].bitcast(FP8X4), rhs_scale=z_s[:, cols], start=True, stop=True,
                )

        b5 = [keep.tile([P, S], F32, name=f"b5_{t}") for t in range(PACK)]
        sg2 = [keep.tile([P, S], F32, name=f"sg2_{t}") for t in range(PACK)]
        prod = [keep.tile([P, S], F32, name=f"prod{t}") for t in range(PACK)]
        res = [keep.tile([P, S], F32, name=f"res{t}") for t in range(PACK)]
        diff = {}
        whole, halves = slice(0, S), (slice(0, HALF), slice(HALF, S))

        def fetch(t, parts):
            col = slice(t, t + 1)
            nc.scalar.copy(out=b_win[t][:, :S], in_=b_ps[t][:])
            nc.scalar.activation(b5[t][:], b_win[t][:].indirect(n5_t[:]), ACT.Copy)
            for cols in parts:
                places = n4_t[:, cols.start // 16 : cols.stop // 16]
                nc.scalar.activation(sg2[t][:, cols], b_win[t][:].indirect(places), ACT.Sigmoid, bias=nb2[:, col], scale=sl2_t[:, col])

        def subtract(t):
            diff[t] = keep.tile([P, S], F32, name=f"diff{t}", tag=f"diff{t % 2}")
            nc.vector.tensor_tensor(diff[t][:], b5[t][:], b_win[t][:, :S], ALU.subtract)

        def multiply(t, cols):
            nc.vector.scalar_tensor_tensor(prod[t][:, cols], a_ps[t][:, cols], 0.0625, sg2[t][:, cols], ALU.mult, ALU.mult)

        def finish(t, cols):
            nc.vector.tensor_tensor(res[t][:, cols], prod[t][:, cols], diff[t][:, cols], ALU.max)
            nc.sync.dma_start(out=out[t * P : (t + 1) * P, cols], in_=res[t][:, cols])

        for t in range(PACK):
            fetch(t, halves if t == PACK - 1 else (whole,))
        subtract(0)
        subtract(1)
        multiply(0, whole)
        multiply(1, whole)
        finish(0, whole)
        subtract(2)
        finish(1, whole)
        multiply(2, whole)
        subtract(3)
        finish(2, whole)
        for cols in halves:
            multiply(3, cols)
        for cols in halves:
            finish(3, cols)
